import numpy as np
import ml_dtypes


def mxq(x, axis, fmt="e4m3"):
    dtype, down = {"e4m3": (ml_dtypes.float8_e4m3fn, 7), "e5m2": (ml_dtypes.float8_e5m2, 14)}[fmt]
    v = np.moveaxis(np.asarray(x, np.float32).astype(ml_dtypes.bfloat16).astype(np.float64), axis, -1)
    blocks = v.reshape(v.shape[:-1] + (-1, 32))
    amax = np.abs(blocks).max(-1, keepdims=True)
    byte = np.maximum(np.where(amax > 0, np.frexp(amax)[1] - 1 + 127, 0) - down, 1)
    scale = np.exp2(byte - 127.0)
    codes = (blocks / scale).astype(np.float32).astype(dtype).astype(np.float64)
    return np.moveaxis((codes * scale).reshape(v.shape), -1, axis)


WIDE = False


def mx_kscale(k):
    if not WIDE:
        return np.ones(k)
    levels = np.array([10, -10, 5, -5, 0])
    if k % 512:
        return np.exp2(np.random.permutation(np.resize(levels, k // 32))).repeat(32)
    a = np.empty((k // 512, 16))
    for p in range(k // 512):
        a[p, :8] = np.random.permutation(np.resize(levels, 8))
        for g in range(8):
            far = levels[np.abs(levels - a[p, g]) >= 10]
            a[p, g + 8] = far[np.random.randint(len(far))]
    return np.exp2(a.ravel()).repeat(32)


def f64(x):
    return np.asarray(x).astype(np.float64)


def striped(idx):
    return np.tile(idx.reshape(-1, 16).T, (8, 1)).astype(np.uint16)


def unstriped(offs):
    return offs[:16].T.reshape(-1).astype(np.int64)


def striped8(idx):
    return np.concatenate([x.reshape(-1, 16).T for x in idx]).astype(np.uint16)


def runs(offs, k):
    lists = np.stack([offs[16 * r : 16 * r + 16].T.reshape(-1) for r in range(8)]).astype(np.int64)
    return lists[np.arange(k) % 512 // 64]


def pack_weight(w):
    k, n = w.shape
    w = f64(np.asarray(w, np.float32).astype(ml_dtypes.bfloat16)).reshape(k // 32, 32, n)
    amax = np.abs(w).max(1)
    byte = np.clip(np.where(amax > 0, np.frexp(amax)[1] - 1 + 127 - 7, 1), 1, 254)
    scaled = (w * np.exp2(127.0 - byte)[:, None, :]).reshape(k, n).astype(np.float32)
    words = np.ascontiguousarray(scaled.reshape(k // 512, 128, 4, n).transpose(0, 1, 3, 2)).astype(ml_dtypes.float8_e4m3fn).view(np.uint8)
    return words, np.ascontiguousarray(byte.astype(np.uint8).reshape(k // 512, 16, n))


def unpack_weight(words, scales):
    g, p, n, _ = words.shape
    vals = np.ascontiguousarray(words).view(ml_dtypes.float8_e4m3fn).astype(np.float64) * np.repeat(np.exp2(scales.astype(np.float64) - 127.0), 8, axis=1)[..., None]
    return vals.transpose(0, 1, 3, 2).reshape(g * 512, n)


def sigmoid(v):
    return 1.0 / (1.0 + np.exp(-np.maximum(v, -700.0)))

def planes(y):
    n, m = y.shape
    v = y.astype(np.float32).astype(ml_dtypes.bfloat16).astype(np.float64).reshape(n // 32, 32, m)
    top = np.abs(v).max(1)
    byte = np.clip(np.where(top > 0, np.frexp(top)[1] - 1 + 127 - 7, 1), 1, 254)
    codes = (v * np.exp2(127.0 - byte)[:, None, :]).reshape(n, m).astype(np.float32).astype(ml_dtypes.float8_e4m3fn).view(np.uint8)
    words = codes.reshape(n // 512, 128, 4, m).transpose(0, 1, 3, 2)
    return np.ascontiguousarray(words), np.ascontiguousarray(byte.astype(np.uint8).reshape(n // 512, 16, m))


K, T, S, N, H = 512, 2048, 512, 512, 512


def setup_inputs():
    n = np.random.standard_normal
    s = mx_kscale(K)[:, None]
    u = mx_kscale(H)
    packed_xT = pack_weight(n((K, T)) * s)
    packed_w1 = pack_weight(n((K, H)) / np.sqrt(K) / s)
    packed_w2 = pack_weight(n((K, H)) / np.sqrt(K) / s)
    packed_w3 = pack_weight(n((H, H)) / np.sqrt(H) / u[:, None])
    packed_w4 = pack_weight(n((H, N)) / np.sqrt(H) / u[:, None])
    return {
        "x_words": packed_xT[0],
        "x_scales": packed_xT[1],
        "w1_words": packed_w1[0],
        "w1_scales": packed_w1[1],
        "w2_words": packed_w2[0],
        "w2_scales": packed_w2[1],
        "gn": (np.random.uniform(0.5, 1.5, (H, 1)) * u[:, None]).astype(np.float32),
        "w3_words": packed_w3[0],
        "w3_scales": packed_w3[1],
        "res": n((N, S)).astype(np.float32),
        "w4_words": packed_w4[0],
        "w4_scales": packed_w4[1],
        "offs": striped(np.random.permutation(T)[:S]),
        "two": striped(np.random.permutation(T)[:S]),
        "pt": striped8(np.stack([np.random.permutation(S) for _ in range(8)])),
        "mv": striped8(np.stack([np.random.permutation(S) for _ in range(8)])),
    }


def reference(x_words, x_scales, w1_words, w1_scales, w2_words, w2_scales, gn, w3_words, w3_scales, res, w4_words, w4_scales, offs, two, pt, mv):
    x_two = unpack_weight(x_words, x_scales)[:, unstriped(two)]
    c = unpack_weight(w2_words, w2_scales).T @ x_two
    xq = unpack_weight(x_words, x_scales)[:, unstriped(offs)]
    y = unpack_weight(w1_words, w1_scales).T @ xq
    z = f64(gn) * (c + (sigmoid(2.0 * (y - (y[np.arange(H)[:, None], runs(pt, H)])))) * (c[np.arange(H)[:, None], runs(pt, H)] - c))
    h = np.tanh(unpack_weight(w3_words, w3_scales).T @ mxq(z, 0, "e4m3"))
    z2 = f64(gn) * (h[np.arange(H)[:, None], runs(mv, H)])
    out_0 = f64(res) + (unpack_weight(w4_words, w4_scales).T @ mxq(z2, 0, "e4m3"))
    return (out_0,) + planes(out_0)

@@ -1,0 +1,249 @@
+from contextlib import ExitStack
+
+import concourse.mybir as mybir
+
+K, T, S, H = 512, 2048, 512, 512
+FLOPS = 4 * 2 * 512 * 512 * 512
+
+F32 = mybir.dt.float32
+BF16 = mybir.dt.bfloat16
+I32 = mybir.dt.int32
+U32 = mybir.dt.uint32
+U16 = mybir.dt.uint16
+U8 = mybir.dt.uint8
+FP8X4 = mybir.dt.float8_e4m3fn_x4
+ACT = mybir.ActivationFunctionType
+ALU = mybir.AluOpType
+
+P = 128
+PACK = 4
+MIX_CHUNKS = [(0, 256), (256, 128), (384, 128)]
+OUT_CHUNKS = [(0, 128), (128, 128), (256, 128), (384, 128)]
+STATES_ON_VECTOR = 0
+PARTNERS_ON_SCALAR = 0
+OWN_ON_VECTOR = 4
+MOVES_ON_VECTOR = (3, 2, 0, 0)
+ROUNDINGS_ON_VECTOR = 1
+
+
+def tile_picked_softswap_none_po_kernel(
+    tc, x_words, x_scales, w1_words, w1_scales, w2_words, w2_scales, gn, w3_words, w3_scales,
+    res, w4_words, w4_scales, offs, two, pt, mv, out_0, out_1, out_2,
+):
+    nc = tc.nc
+    with ExitStack() as ctx:
+        lists = ctx.enter_context(tc.tile_pool(name="lists", bufs=1))
+        sb = ctx.enter_context(tc.tile_pool(name="sb", bufs=1))
+        shared = ctx.enter_context(tc.tile_pool(name="shared", bufs=1))
+        psum = ctx.enter_context(tc.psum_pool(name="psum", bufs=1))
+
+        def tile(name, shape, dtype, tag=None):
+            return sb.tile(shape, dtype, name=name, tag=tag or name, align_bytes=64)
+
+        def placed(name, shape, dtype, offset):
+            return shared.tile(shape, dtype, name=name, offset=offset, align_bytes=64)
+
+        def load_list(name, source):
+            held = lists.tile([P, S // 16], U16, name=name)
+            nc.sync.dma_start(held[:], source)
+            return held
+
+        def load_words(queue, name, source, width, tag):
+            held = tile(name, [P, width], U32, tag=tag)
+            queue.dma_start(held[:].bitcast(I32), source[0].rearrange("p n t -> p (n t)").bitcast(I32))
+            return held
+
+        def load_scale_rows(queue, held, first_row, source):
+            for quad in range(4):
+                row = 32 * quad + first_row
+                queue.dma_start(held[row : row + 4, :].bitcast(I32), source[0, 4 * quad : 4 * quad + 4, :].bitcast(I32))
+
+        def deal_words(name, raw):
+            dealt = tile(name, [P, H], U32)
+            nc.scalar.copy(
+                dealt[:].rearrange("p (t b i) -> p b t i", t=PACK, i=4),
+                raw[:].rearrange("p (b i t) -> p b t i", t=PACK, i=4),
+            )
+            return dealt
+
+        def deal_scales(name, raw):
+            dealt = tile(name, [P, H], U8)
+            nc.vector.tensor_copy(
+                dealt[:].rearrange("p (t m) -> p t m", t=PACK), raw[:].rearrange("p (m t) -> p t m", t=PACK)
+            )
+            return dealt
+
+        def product(out, weight, t, codes, scales):
+            words, plane, first_row = weight
+            cols = slice(t * P, (t + 1) * P)
+            nc.tensor.matmul_mx(
+                out=out, lhsT=words[:, cols].bitcast(FP8X4), lhsT_scale=plane[first_row:P, cols],
+                rhs=codes.bitcast(FP8X4), rhs_scale=scales, start=True, stop=True,
+            )
+
+        def woven(rounded):
+            return rounded[:].rearrange("p (c i t) -> p c t i", i=2, t=PACK)
+
+        def by_pairs(planes):
+            return planes[:].rearrange("p t (c i) -> p c t i", i=2)
+
+        def entries(held, first, width):
+            return held[:, first // 16 : (first + width) // 16]
+
+        xs_raw = tile("xs_raw", [P, T], U8)
+        ws1_raw = placed("ws1_raw", [P, H], U8, 256)
+        nc.gpsimd.memset(ws1_raw[:].bitcast(I32), 0)
+        nc.gpsimd.memset(xs_raw[:].bitcast(I32), 0)
+        load_scale_rows(nc.gpsimd, ws1_raw, 0, w1_scales)
+        ws2_raw = tile("ws2_raw", [P, H], U8, tag="ws_raw")
+        nc.gpsimd.memset(ws2_raw[:].bitcast(I32), 0)
+
+        offs_t = load_list("offs_t", offs)
+        two_t = load_list("two_t", two)
+        pt_t = load_list("pt_t", pt)
+        mv_t = load_list("mv_t", mv)
+        xw_raw = load_words(nc.sync, "xw_raw", x_words, T, "wide_raw")
+        w1_raw = load_words(nc.sync, "w1_raw", w1_words, H, "w13_raw")
+        w2_raw = load_words(nc.sync, "w2_raw", w2_words, H, "w24_raw")
+        load_scale_rows(nc.scalar, xs_raw, 0, x_scales)
+        load_scale_rows(nc.sync, ws2_raw, 0, w2_scales)
+        gain = tile("gain", [P, PACK], F32)
+        nc.gpsimd.dma_start(gain[:], gn.rearrange("(p t) o -> p (t o)", t=PACK))
+        half_gain = tile("half_gain", [P, PACK], F32)
+        nc.gpsimd.tensor_scalar(half_gain[:], gain[:], 0.5, 0.0, ALU.mult, ALU.add)
+
+        xs_y = tile("xs_y", [P, S], U8)
+        xw_y = tile("xw_y", [P, S], U32, tag="words_y")
+        nc.vector.tensor_copy(xw_y[:], xw_raw[:].indirect(offs_t[:]))
+        nc.vector.tensor_copy(xs_y[:], xs_raw[:].indirect(offs_t[:]))
+        w1 = (deal_words("w1_d", w1_raw), deal_scales("ws1", ws1_raw), 0)
+        xs_c = placed("xs_c", [P, S], U8, 0)
+        xw_c = placed("xw_c", [P, S], U32, 512)
+        nc.vector.tensor_copy(xw_c[:], xw_raw[:].indirect(two_t[:]))
+        nc.vector.tensor_copy(xs_c[:], xs_raw[:].indirect(two_t[:]))
+        w2 = (deal_words("w2_d", w2_raw), deal_scales("ws2", ws2_raw), 0)
+
+        ws34_raw = tile("ws34_raw", [P, H], U8, tag="ws_raw")
+        nc.gpsimd.memset(ws34_raw[:].bitcast(I32), 0)
+        load_scale_rows(nc.sync, ws34_raw, 0, w3_scales)
+        load_scale_rows(nc.sync, ws34_raw, 4, w4_scales)
+
+        y_ps = [psum.tile([P, S], F32, name=f"y_ps{t}", tag=f"bank_y{t}") for t in range(PACK)]
+        c_ps = [psum.tile([P, S], F32, name=f"c_ps{t}", tag=f"bank_c{t}") for t in range(PACK)]
+        for t in range(PACK):
+            product(y_ps[t][:], w1, t, xw_y[:], xs_y[:])
+        for t in range(PACK):
+            product(c_ps[t][:], w2, t, xw_c[:], xs_c[:])
+
+        w3_raw = load_words(nc.sync, "w3_raw", w3_words, H, "words_y")
+        y_win = [tile(f"y_win{t}", [P, S], F32) for t in range(PACK)]
+        c_win = [tile(f"c_win{t}", [P, S], F32) for t in range(PACK)]
+        h_win = [tile(f"h_win{t}", [P, S], F32) for t in range(PACK)]
+        y_own = [tile(f"y_own{t}", [P, S], F32, tag=f"own{t}") for t in range(PACK)]
+        a_ps = {}
+        w3 = None
+        w4 = None
+
+        for n, (first, width) in enumerate(MIX_CHUNKS):
+            cols = slice(first, first + width)
+            partner_c = tile(f"partner_c{n}", [P, PACK, width], F32)
+            gap = tile(f"gap{n}", [P, PACK, width], F32)
+            pull = tile(f"pull{n}", [P, PACK, width], F32)
+            taken = tile(f"taken{n}", [P, PACK, width], F32)
+            kept = tile(f"kept{n}", [P, PACK, width], F32)
+            if n == 0:
+                for t in range(PACK):
+                    nc.scalar.copy(y_win[t][:], y_ps[t][:])
+                    if t >= OWN_ON_VECTOR:
+                        nc.sync.dma_start(y_own[t][:], y_win[t][:])
+            for t in range(PACK):
+                if n == 0 and t < OWN_ON_VECTOR:
+                    nc.vector.tensor_copy(y_own[t][:], y_win[t][:])
+                if n == 0 and t < STATES_ON_VECTOR:
+                    nc.vector.tensor_scalar(c_win[t][:], c_ps[t][:], half_gain[:, t : t + 1], None, ALU.mult)
+                if n == 0 and t >= STATES_ON_VECTOR:
+                    nc.scalar.activation(c_win[t][:], c_ps[t][:], ACT.Copy, scale=half_gain[:, t : t + 1])
+                partners = entries(pt_t, first, width)
+                nc.vector.tensor_tensor(gap[:, t, :], y_win[t][:].indirect(partners), y_own[t][:, cols], ALU.subtract)
+                nc.scalar.activation(pull[:, t, :], gap[:, t, :], ACT.Tanh)
+                nc.vector.scalar_tensor_tensor(
+                    kept[:, t, :], pull[:, t, :], 1.0, c_win[t][:, cols], ALU.add, ALU.mult
+                )
+                nc.scalar.activation(partner_c[:, t, :], c_win[t][:].indirect(partners), ACT.Copy)
+                nc.vector.scalar_tensor_tensor(
+                    taken[:, t, :], pull[:, t, :], 1.0, partner_c[:, t, :], ALU.subtract, ALU.mult
+                )
+            if n == 0:
+                ws34 = deal_scales("ws34", ws34_raw)
+                w3 = (deal_words("w3_d", w3_raw), ws34, 0)
+            z_bf = tile(f"z_bf{n}", [P, PACK * width], BF16)
+            nc.vector.tensor_tensor(woven(z_bf), by_pairs(kept), by_pairs(taken), ALU.subtract)
+            z_words = tile(f"z_words{n}", [P, width], U32)
+            z_scales = tile(f"z_scales{n}", [P, width], U8)
+            nc.vector.quantize_mx(out=z_words[:].bitcast(FP8X4), scales=z_scales[:], in_=z_bf[:])
+            for t in range(PACK):
+                bank = f"bank_c{t}" if n % 2 == 0 else f"bank_y{t}"
+                a_ps[n, t] = psum.tile([P, width], F32, name=f"a_ps{n}_{t}", tag=bank)
+                product(a_ps[n, t][:], w3, t, z_words[:], z_scales[:])
+        for n, (first, width) in enumerate(MIX_CHUNKS):
+            cols = slice(first, first + width)
+            for t in range(PACK):
+                nc.scalar.activation(h_win[t][:, cols], a_ps[n, t][:], ACT.Tanh)
+                if n < 2:
+                    nc.scalar.activation(h_win[t][:, cols], h_win[t][:, cols], ACT.Copy, scale=gain[:, t : t + 1])
+                else:
+                    nc.vector.tensor_scalar(h_win[t][:, cols], h_win[t][:, cols], gain[:, t : t + 1], None, ALU.mult)
+            if n == 0:
+                w4_raw = load_words(nc.sync, "w4_raw", w4_words, H, "words_y")
+                w4 = (deal_words("w4_d", w4_raw), ws34, 4)
+
+        out_rows = out_0.rearrange("(p t) j -> p t j", t=PACK)
+        out_words = out_1[0].rearrange("p n t -> p (n t)").bitcast(I32)
+        o_ps = {}
+        o_words = tile("o_words", [P, S], U32)
+        o_scales = tile("o_scales", [P, S], U8)
+        for n, (first, width) in enumerate(OUT_CHUNKS):
+            cols = slice(first, first + width)
+            moved = tile(f"moved{n}", [P, PACK, width], F32)
+            for t in range(PACK):
+                looked_up = h_win[t][:].indirect(entries(mv_t, first, width))
+                if t < MOVES_ON_VECTOR[n]:
+                    nc.vector.tensor_copy(moved[:, t, :], looked_up)
+                else:
+                    nc.scalar.activation(moved[:, t, :], looked_up, ACT.Copy)
+            z2_bf = tile(f"z2_bf{n}", [P, PACK * width], BF16)
+            nc.vector.tensor_copy(woven(z2_bf), by_pairs(moved))
+            z2_words = tile(f"z2_words{n}", [P, width], U32)
+            z2_scales = tile(f"z2_scales{n}", [P, width], U8)
+            nc.vector.quantize_mx(out=z2_words[:].bitcast(FP8X4), scales=z2_scales[:], in_=z2_bf[:])
+            halves = max(1, width // P)
+            per = PACK // halves
+            for half in range(halves):
+                o_ps[n, half] = psum.tile([P, per, width], F32, name=f"o_ps{n}_{half}", tag=f"bank_y{(first // P + half) % PACK}")
+                for t in range(per):
+                    product(o_ps[n, half][:, t, :], w4, half * per + t, z2_words[:], z2_scales[:])
+        for n, (first, width) in enumerate(OUT_CHUNKS):
+            cols = slice(first, first + width)
+            res_t = tile(f"res{n}", [P, PACK, width], F32, tag=f"own{n}")
+            nc.sync.dma_start(res_t[:], res.rearrange("(p t) j -> p t j", t=PACK)[:, :, cols])
+            halves = max(1, width // P)
+            per = PACK // halves
+            result = tile(f"result{n}", [P, PACK, width], F32)
+            for half in range(halves):
+                rows = slice(half * per, (half + 1) * per)
+                nc.vector.tensor_tensor(result[:, rows, :], o_ps[n, half][:], res_t[:, rows, :], ALU.add)
+            nc.sync.dma_start(out_rows[:, :, cols], result[:])
+            o_bf = tile(f"o_bf{n}", [P, PACK * width], BF16)
+            if n >= len(OUT_CHUNKS) - ROUNDINGS_ON_VECTOR:
+                nc.vector.tensor_copy(woven(o_bf), by_pairs(result))
+            else:
+                nc.scalar.copy(woven(o_bf), by_pairs(result))
+            nc.vector.quantize_mx(out=o_words[:, cols].bitcast(FP8X4), scales=o_scales[:, cols], in_=o_bf[:])
+            if n >= len(OUT_CHUNKS) - 2:
+                stored = slice(first if n == len(OUT_CHUNKS) - 1 else 0, first + width)
+                nc.sync.dma_start(out_words[:, stored], o_words[:, stored].bitcast(I32))
+        for quad in range(4):
+            queue = nc.scalar if quad % 2 else nc.sync
+            queue.dma_start(
+                out_2[0, 4 * quad : 4 * quad + 4, :].bitcast(I32), o_scales[32 * quad : 32 * quad + 4, :].bitcast(I32)
+            )

@@ -21,6 +21,9 @@ MIX_CHUNKS = [(0, 256), (256, 128), (384, 128)]
 OUT_CHUNKS = [(0, 128), (128, 128), (256, 128), (384, 128)]
 STATES_ON_VECTOR = 0
 PARTNERS_ON_SCALAR = 0
+GROUP = (2, 2, 2)
+LEAD = 1
+OWN_ON_SCALAR = 1
 OWN_ON_VECTOR = 4
 MOVES_ON_VECTOR = (3, 2, 0, 0)
 ROUNDINGS_ON_VECTOR = 1
@@ -53,8 +56,8 @@ def tile_picked_softswap_none_po_kernel(
             queue.dma_start(held[:].bitcast(I32), source[0].rearrange("p n t -> p (n t)").bitcast(I32))
             return held
 
-        def load_scale_rows(queue, held, first_row, source):
-            for quad in range(4):
+        def load_scale_rows(queues, held, first_row, source):
+            for quad, queue in enumerate(queues):
                 row = 32 * quad + first_row
                 queue.dma_start(held[row : row + 4, :].bitcast(I32), source[0, 4 * quad : 4 * quad + 4, :].bitcast(I32))
 
@@ -92,27 +95,22 @@ def tile_picked_softswap_none_po_kernel(
 
         xs_raw = tile("xs_raw", [P, T], U8)
         ws1_raw = placed("ws1_raw", [P, H], U8, 256)
-        nc.gpsimd.memset(ws1_raw[:].bitcast(I32), 0)
+        ws2_raw = tile("ws2_raw", [P, H], U8, tag="ws2_own_res")
         nc.gpsimd.memset(xs_raw[:].bitcast(I32), 0)
-        load_scale_rows(nc.gpsimd, ws1_raw, 0, w1_scales)
-        ws2_raw = tile("ws2_raw", [P, H], U8, tag="ws_raw")
+        nc.gpsimd.memset(ws1_raw[:].bitcast(I32), 0)
         nc.gpsimd.memset(ws2_raw[:].bitcast(I32), 0)
-
+        xw_raw = load_words(nc.scalar, "xw_raw", x_words, T, "xw_raw")
         offs_t = load_list("offs_t", offs)
+        w1_raw = load_words(nc.sync, "w1_raw", w1_words, H, "w1_then_gain")
         two_t = load_list("two_t", two)
         pt_t = load_list("pt_t", pt)
         mv_t = load_list("mv_t", mv)
-        xw_raw = load_words(nc.sync, "xw_raw", x_words, T, "wide_raw")
-        w1_raw = load_words(nc.sync, "w1_raw", w1_words, H, "w13_raw")
-        w2_raw = load_words(nc.sync, "w2_raw", w2_words, H, "w24_raw")
-        load_scale_rows(nc.scalar, xs_raw, 0, x_scales)
-        load_scale_rows(nc.sync, ws2_raw, 0, w2_scales)
-        gain = tile("gain", [P, PACK], F32)
-        nc.gpsimd.dma_start(gain[:], gn.rearrange("(p t) o -> p (t o)", t=PACK))
-        half_gain = tile("half_gain", [P, PACK], F32)
-        nc.gpsimd.tensor_scalar(half_gain[:], gain[:], 0.5, 0.0, ALU.mult, ALU.add)
+        w2_raw = load_words(nc.sync, "w2_raw", w2_words, H, "w2_raw")
+        load_scale_rows([nc.scalar, nc.gpsimd, nc.gpsimd, nc.gpsimd], xs_raw, 0, x_scales)
+        load_scale_rows([nc.sync] * 4, ws1_raw, 0, w1_scales)
+        load_scale_rows([nc.sync] * 4, ws2_raw, 0, w2_scales)
 
-        xs_y = tile("xs_y", [P, S], U8)
+        xs_y = tile("xs_y", [P, S], U8, tag="xs_y_then_ws34")
         xw_y = tile("xw_y", [P, S], U32, tag="words_y")
         nc.vector.tensor_copy(xw_y[:], xw_raw[:].indirect(offs_t[:]))
         nc.vector.tensor_copy(xs_y[:], xs_raw[:].indirect(offs_t[:]))
@@ -123,10 +121,10 @@ def tile_picked_softswap_none_po_kernel(
         nc.vector.tensor_copy(xs_c[:], xs_raw[:].indirect(two_t[:]))
         w2 = (deal_words("w2_d", w2_raw), deal_scales("ws2", ws2_raw), 0)
 
-        ws34_raw = tile("ws34_raw", [P, H], U8, tag="ws_raw")
-        nc.gpsimd.memset(ws34_raw[:].bitcast(I32), 0)
-        load_scale_rows(nc.sync, ws34_raw, 0, w3_scales)
-        load_scale_rows(nc.sync, ws34_raw, 4, w4_scales)
+        gain = tile("gain", [P, PACK], F32, tag="w1_then_gain")
+        nc.sync.dma_start(gain[:], gn.rearrange("(p t) o -> p (t o)", t=PACK))
+        half_gain = tile("half_gain", [P, PACK], F32)
+        nc.scalar.activation(half_gain[:], gain[:], ACT.Copy, scale=0.5)
 
         y_ps = [psum.tile([P, S], F32, name=f"y_ps{t}", tag=f"bank_y{t}") for t in range(PACK)]
         c_ps = [psum.tile([P, S], F32, name=f"c_ps{t}", tag=f"bank_c{t}") for t in range(PACK)]
@@ -136,48 +134,54 @@ def tile_picked_softswap_none_po_kernel(
             product(c_ps[t][:], w2, t, xw_c[:], xs_c[:])
 
         w3_raw = load_words(nc.sync, "w3_raw", w3_words, H, "words_y")
+        ws34_raw = tile("ws34_raw", [P, H], U8, tag="xs_y_then_ws34")
+        nc.vector.memset(ws34_raw[:].bitcast(I32), 0)
+        load_scale_rows([nc.sync] * 4, ws34_raw, 0, w3_scales)
+        load_scale_rows([nc.sync] * 4, ws34_raw, 4, w4_scales)
         y_win = [tile(f"y_win{t}", [P, S], F32) for t in range(PACK)]
         c_win = [tile(f"c_win{t}", [P, S], F32) for t in range(PACK)]
         h_win = [tile(f"h_win{t}", [P, S], F32) for t in range(PACK)]
-        y_own = [tile(f"y_own{t}", [P, S], F32, tag=f"own{t}") for t in range(PACK)]
+        y_own = tile("y_own", [P, PACK, S], F32, tag="ws2_own_res")
         a_ps = {}
         w3 = None
         w4 = None
 
-        for n, (first, width) in enumerate(MIX_CHUNKS):
-            cols = slice(first, first + width)
-            partner_c = tile(f"partner_c{n}", [P, PACK, width], F32)
-            gap = tile(f"gap{n}", [P, PACK, width], F32)
-            pull = tile(f"pull{n}", [P, PACK, width], F32)
-            taken = tile(f"taken{n}", [P, PACK, width], F32)
-            kept = tile(f"kept{n}", [P, PACK, width], F32)
-            if n == 0:
-                for t in range(PACK):
-                    nc.scalar.copy(y_win[t][:], y_ps[t][:])
-                    if t >= OWN_ON_VECTOR:
-                        nc.sync.dma_start(y_own[t][:], y_win[t][:])
-            for t in range(PACK):
-                if n == 0 and t < OWN_ON_VECTOR:
-                    nc.vector.tensor_copy(y_own[t][:], y_win[t][:])
-                if n == 0 and t < STATES_ON_VECTOR:
-                    nc.vector.tensor_scalar(c_win[t][:], c_ps[t][:], half_gain[:, t : t + 1], None, ALU.mult)
-                if n == 0 and t >= STATES_ON_VECTOR:
-                    nc.scalar.activation(c_win[t][:], c_ps[t][:], ACT.Copy, scale=half_gain[:, t : t + 1])
-                partners = entries(pt_t, first, width)
-                nc.vector.tensor_tensor(gap[:, t, :], y_win[t][:].indirect(partners), y_own[t][:, cols], ALU.subtract)
-                nc.scalar.activation(pull[:, t, :], gap[:, t, :], ACT.Tanh)
+        partner_c, gap, pull = {}, {}, {}
+
+        def look_up(n, t):
+            first, width = MIX_CHUNKS[n]
+            if t == 0:
+                partner_c[n] = tile(f"partner_c{n}", [P, PACK, width], F32)
+                gap[n] = tile(f"gap{n}", [P, PACK, width], F32)
+                pull[n] = tile(f"pull{n}", [P, PACK, width], F32)
+            partners = entries(pt_t, first, width)
+            own = y_own[:, t, first : first + width]
+            nc.vector.tensor_tensor(gap[n][:, t, :], y_win[t][:].indirect(partners), own, ALU.subtract)
+            if (t + 1) % GROUP[n] == 0:
+                group = slice(t + 1 - GROUP[n], t + 1)
+                nc.scalar.activation(pull[n][:, group, :], gap[n][:, group, :], ACT.Tanh)
+            nc.scalar.activation(partner_c[n][:, t, :], c_win[t][:].indirect(partners), ACT.Copy)
+
+        taken, kept = {}, {}
+
+        def weigh(n, t):
+            first, width = MIX_CHUNKS[n]
+            if t == 0:
+                taken[n] = tile(f"taken{n}", [P, PACK, width], F32)
+                kept[n] = tile(f"kept{n}", [P, PACK, width], F32)
+            nc.vector.scalar_tensor_tensor(
+                kept[n][:, t, :], pull[n][:, t, :], 1.0, c_win[t][:, first : first + width], ALU.add, ALU.mult
+            )
+            if (t + 1) % GROUP[n] == 0:
+                group = slice(t + 1 - GROUP[n], t + 1)
                 nc.vector.scalar_tensor_tensor(
-                    kept[:, t, :], pull[:, t, :], 1.0, c_win[t][:, cols], ALU.add, ALU.mult
+                    taken[n][:, group, :], pull[n][:, group, :], 1.0, partner_c[n][:, group, :], ALU.subtract, ALU.mult
                 )
-                nc.scalar.activation(partner_c[:, t, :], c_win[t][:].indirect(partners), ACT.Copy)
-                nc.vector.scalar_tensor_tensor(
-                    taken[:, t, :], pull[:, t, :], 1.0, partner_c[:, t, :], ALU.subtract, ALU.mult
-                )
-            if n == 0:
-                ws34 = deal_scales("ws34", ws34_raw)
-                w3 = (deal_words("w3_d", w3_raw), ws34, 0)
+
+        def mix(n):
+            first, width = MIX_CHUNKS[n]
             z_bf = tile(f"z_bf{n}", [P, PACK * width], BF16)
-            nc.vector.tensor_tensor(woven(z_bf), by_pairs(kept), by_pairs(taken), ALU.subtract)
+            nc.vector.tensor_tensor(woven(z_bf), by_pairs(kept[n]), by_pairs(taken[n]), ALU.subtract)
             z_words = tile(f"z_words{n}", [P, width], U32)
             z_scales = tile(f"z_scales{n}", [P, width], U8)
             nc.vector.quantize_mx(out=z_words[:].bitcast(FP8X4), scales=z_scales[:], in_=z_bf[:])
@@ -185,11 +189,33 @@ def tile_picked_softswap_none_po_kernel(
                 bank = f"bank_c{t}" if n % 2 == 0 else f"bank_y{t}"
                 a_ps[n, t] = psum.tile([P, width], F32, name=f"a_ps{n}_{t}", tag=bank)
                 product(a_ps[n, t][:], w3, t, z_words[:], z_scales[:])
+
+        for t in range(PACK):
+            nc.scalar.copy(y_win[t][:], y_ps[t][:])
+        for t in range(PACK):
+            if t >= PACK - OWN_ON_SCALAR:
+                nc.scalar.copy(y_own[:, t, :], y_ps[t][:])
+            else:
+                nc.vector.tensor_copy(y_own[:, t, :], y_win[t][:])
+        units = [(n, t) for n in range(len(MIX_CHUNKS)) for t in range(PACK)]
+        for step in range(len(units) + LEAD):
+            if step < PACK:
+                nc.scalar.activation(c_win[step][:], c_ps[step][:], ACT.Copy, scale=half_gain[:, step : step + 1])
+            if step < len(units):
+                look_up(*units[step])
+            if step == PACK:
+                ws34 = deal_scales("ws34", ws34_raw)
+                w3 = (deal_words("w3_d", w3_raw), ws34, 0)
+            if step >= LEAD:
+                n, t = units[step - LEAD]
+                weigh(n, t)
+                if t == PACK - 1:
+                    mix(n)
         for n, (first, width) in enumerate(MIX_CHUNKS):
             cols = slice(first, first + width)
             for t in range(PACK):
                 nc.scalar.activation(h_win[t][:, cols], a_ps[n, t][:], ACT.Tanh)
-                if n < 2:
+                if n < 1:
                     nc.scalar.activation(h_win[t][:, cols], h_win[t][:, cols], ACT.Copy, scale=gain[:, t : t + 1])
                 else:
                     nc.vector.tensor_scalar(h_win[t][:, cols], h_win[t][:, cols], gain[:, t : t + 1], None, ALU.mult)
@@ -197,6 +223,8 @@ def tile_picked_softswap_none_po_kernel(
                 w4_raw = load_words(nc.sync, "w4_raw", w4_words, H, "words_y")
                 w4 = (deal_words("w4_d", w4_raw), ws34, 4)
 
+        res_t = tile("res_t", [P, PACK, S], F32, tag="ws2_own_res")
+        nc.sync.dma_start(res_t[:], res.rearrange("(p t) j -> p t j", t=PACK))
         out_rows = out_0.rearrange("(p t) j -> p t j", t=PACK)
         out_words = out_1[0].rearrange("p n t -> p (n t)").bitcast(I32)
         o_ps = {}
@@ -224,14 +252,12 @@ def tile_picked_softswap_none_po_kernel(
                     product(o_ps[n, half][:, t, :], w4, half * per + t, z2_words[:], z2_scales[:])
         for n, (first, width) in enumerate(OUT_CHUNKS):
             cols = slice(first, first + width)
-            res_t = tile(f"res{n}", [P, PACK, width], F32, tag=f"own{n}")
-            nc.sync.dma_start(res_t[:], res.rearrange("(p t) j -> p t j", t=PACK)[:, :, cols])
             halves = max(1, width // P)
             per = PACK // halves
             result = tile(f"result{n}", [P, PACK, width], F32)
             for half in range(halves):
                 rows = slice(half * per, (half + 1) * per)
-                nc.vector.tensor_tensor(result[:, rows, :], o_ps[n, half][:], res_t[:, rows, :], ALU.add)
+                nc.vector.tensor_tensor(result[:, rows, :], o_ps[n, half][:], res_t[:, rows, cols], ALU.add)
             nc.sync.dma_start(out_rows[:, :, cols], result[:])
             o_bf = tile(f"o_bf{n}", [P, PACK * width], BF16)
             if n >= len(OUT_CHUNKS) - ROUNDINGS_ON_VECTOR:

@@ -17,15 +17,16 @@ ALU = mybir.AluOpType
 
 P = 128
 PACK = 4
-MIX_CHUNKS = [(0, 256), (256, 128), (384, 128)]
+MIX_CHUNKS = [(0, 256), (256, 256)]
 OUT_CHUNKS = [(0, 128), (128, 128), (256, 128), (384, 128)]
 STATES_ON_VECTOR = 0
 PARTNERS_ON_SCALAR = 0
-GROUP = (2, 2, 2)
+GROUP = (2, 2)
+SPLIT = (1, 2)
 LEAD = 1
-OWN_ON_SCALAR = 1
+OWN_ON_SCALAR = 2
 OWN_ON_VECTOR = 4
-MOVES_ON_VECTOR = (3, 2, 0, 0)
+MOVES_ON_VECTOR = (1, 1, 1, 1)
 ROUNDINGS_ON_VECTOR = 1
 
 
@@ -99,15 +100,15 @@ def tile_picked_softswap_none_po_kernel(
         nc.gpsimd.memset(xs_raw[:].bitcast(I32), 0)
         nc.gpsimd.memset(ws1_raw[:].bitcast(I32), 0)
         nc.gpsimd.memset(ws2_raw[:].bitcast(I32), 0)
-        xw_raw = load_words(nc.scalar, "xw_raw", x_words, T, "xw_raw")
         offs_t = load_list("offs_t", offs)
-        w1_raw = load_words(nc.sync, "w1_raw", w1_words, H, "w1_then_gain")
         two_t = load_list("two_t", two)
         pt_t = load_list("pt_t", pt)
         mv_t = load_list("mv_t", mv)
+        xw_raw = load_words(nc.sync, "xw_raw", x_words, T, "xw_raw")
+        w1_raw = load_words(nc.sync, "w1_raw", w1_words, H, "w1_then_gain")
         w2_raw = load_words(nc.sync, "w2_raw", w2_words, H, "w2_raw")
-        load_scale_rows([nc.scalar, nc.gpsimd, nc.gpsimd, nc.gpsimd], xs_raw, 0, x_scales)
-        load_scale_rows([nc.sync] * 4, ws1_raw, 0, w1_scales)
+        load_scale_rows([nc.scalar] * 4, xs_raw, 0, x_scales)
+        load_scale_rows([nc.sync, nc.sync, nc.gpsimd, nc.gpsimd], ws1_raw, 0, w1_scales)
         load_scale_rows([nc.sync] * 4, ws2_raw, 0, w2_scales)
 
         xs_y = tile("xs_y", [P, S], U8, tag="xs_y_then_ws34")
@@ -178,17 +179,29 @@ def tile_picked_softswap_none_po_kernel(
                     taken[n][:, group, :], pull[n][:, group, :], 1.0, partner_c[n][:, group, :], ALU.subtract, ALU.mult
                 )
 
+        pieces = []
+
         def mix(n):
             first, width = MIX_CHUNKS[n]
-            z_bf = tile(f"z_bf{n}", [P, PACK * width], BF16)
-            nc.vector.tensor_tensor(woven(z_bf), by_pairs(kept[n]), by_pairs(taken[n]), ALU.subtract)
-            z_words = tile(f"z_words{n}", [P, width], U32)
-            z_scales = tile(f"z_scales{n}", [P, width], U8)
-            nc.vector.quantize_mx(out=z_words[:].bitcast(FP8X4), scales=z_scales[:], in_=z_bf[:])
-            for t in range(PACK):
-                bank = f"bank_c{t}" if n % 2 == 0 else f"bank_y{t}"
-                a_ps[n, t] = psum.tile([P, width], F32, name=f"a_ps{n}_{t}", tag=bank)
-                product(a_ps[n, t][:], w3, t, z_words[:], z_scales[:])
+            part = width // SPLIT[n]
+            rounded = []
+            for start in range(0, width, part):
+                z_bf = tile(f"z_bf{first + start}", [P, PACK * part], BF16)
+                within = slice(start // 2, (start + part) // 2)
+                nc.vector.tensor_tensor(
+                    woven(z_bf), by_pairs(kept[n])[:, within], by_pairs(taken[n])[:, within], ALU.subtract
+                )
+                rounded.append(z_bf)
+            for z_bf, start in zip(rounded, range(first, first + width, part)):
+                z_words = tile(f"z_words{start}", [P, part], U32)
+                z_scales = tile(f"z_scales{start}", [P, part], U8)
+                nc.vector.quantize_mx(out=z_words[:].bitcast(FP8X4), scales=z_scales[:], in_=z_bf[:])
+                piece = len(pieces)
+                pieces.append((start, part))
+                for t in range(PACK):
+                    bank = f"bank_c{t}" if piece % 2 == 0 else f"bank_y{t}"
+                    a_ps[piece, t] = psum.tile([P, part], F32, name=f"a_ps{piece}_{t}", tag=bank)
+                    product(a_ps[piece, t][:], w3, t, z_words[:], z_scales[:])
 
         for t in range(PACK):
             nc.scalar.copy(y_win[t][:], y_ps[t][:])
@@ -211,14 +224,15 @@ def tile_picked_softswap_none_po_kernel(
                 weigh(n, t)
                 if t == PACK - 1:
                     mix(n)
-        for n, (first, width) in enumerate(MIX_CHUNKS):
+        for n, (first, width) in enumerate(pieces):
             cols = slice(first, first + width)
             for t in range(PACK):
                 nc.scalar.activation(h_win[t][:, cols], a_ps[n, t][:], ACT.Tanh)
-                if n < 1:
+                if n == 0:
                     nc.scalar.activation(h_win[t][:, cols], h_win[t][:, cols], ACT.Copy, scale=gain[:, t : t + 1])
-                else:
-                    nc.vector.tensor_scalar(h_win[t][:, cols], h_win[t][:, cols], gain[:, t : t + 1], None, ALU.mult)
+                if n == len(pieces) - 1:
+                    late = slice(pieces[1][0], S)
+                    nc.vector.tensor_scalar(h_win[t][:, late], h_win[t][:, late], gain[:, t : t + 1], None, ALU.mult)
             if n == 0:
                 w4_raw = load_words(nc.sync, "w4_raw", w4_words, H, "words_y")
                 w4 = (deal_words("w4_d", w4_raw), ws34, 4)

@@ -95,31 +95,32 @@ def tile_picked_softswap_none_po_kernel(
             return held[:, first // 16 : (first + width) // 16]
 
         xs_raw = tile("xs_raw", [P, T], U8)
-        ws1_raw = placed("ws1_raw", [P, H], U8, 256)
+        ws1_raw = tile("ws1_raw", [P, H], U8, tag="ws1_then_words_c")
         ws2_raw = tile("ws2_raw", [P, H], U8, tag="ws2_own_res")
-        nc.gpsimd.memset(xs_raw[:].bitcast(I32), 0)
+        nc.gpsimd.memset(xs_raw[:, : T // 2].bitcast(I32), 0)
+        nc.vector.memset(xs_raw[:, T // 2 :].bitcast(I32), 0)
         nc.gpsimd.memset(ws1_raw[:].bitcast(I32), 0)
         nc.gpsimd.memset(ws2_raw[:].bitcast(I32), 0)
         offs_t = load_list("offs_t", offs)
         two_t = load_list("two_t", two)
         pt_t = load_list("pt_t", pt)
-        mv_t = load_list("mv_t", mv)
+        load_scale_rows([nc.sync] * 4, xs_raw, 0, x_scales)
         xw_raw = load_words(nc.sync, "xw_raw", x_words, T, "xw_raw")
+        mv_t = load_list("mv_t", mv)
         w1_raw = load_words(nc.sync, "w1_raw", w1_words, H, "w1_then_gain")
+        load_scale_rows([nc.sync] * 4, ws1_raw, 0, w1_scales)
         w2_raw = load_words(nc.sync, "w2_raw", w2_words, H, "w2_raw")
-        load_scale_rows([nc.scalar] * 4, xs_raw, 0, x_scales)
-        load_scale_rows([nc.sync, nc.sync, nc.gpsimd, nc.gpsimd], ws1_raw, 0, w1_scales)
         load_scale_rows([nc.sync] * 4, ws2_raw, 0, w2_scales)
 
         xs_y = tile("xs_y", [P, S], U8, tag="xs_y_then_ws34")
         xw_y = tile("xw_y", [P, S], U32, tag="words_y")
-        nc.vector.tensor_copy(xw_y[:], xw_raw[:].indirect(offs_t[:]))
+        xs_c = tile("xs_c", [P, S], U8)
         nc.vector.tensor_copy(xs_y[:], xs_raw[:].indirect(offs_t[:]))
-        w1 = (deal_words("w1_d", w1_raw), deal_scales("ws1", ws1_raw), 0)
-        xs_c = placed("xs_c", [P, S], U8, 0)
-        xw_c = placed("xw_c", [P, S], U32, 512)
-        nc.vector.tensor_copy(xw_c[:], xw_raw[:].indirect(two_t[:]))
         nc.vector.tensor_copy(xs_c[:], xs_raw[:].indirect(two_t[:]))
+        nc.vector.tensor_copy(xw_y[:], xw_raw[:].indirect(offs_t[:]))
+        w1 = (deal_words("w1_d", w1_raw), deal_scales("ws1", ws1_raw), 0)
+        xw_c = tile("xw_c", [P, S], U32, tag="ws1_then_words_c")
+        nc.vector.tensor_copy(xw_c[:], xw_raw[:].indirect(two_t[:]))
         w2 = (deal_words("w2_d", w2_raw), deal_scales("ws2", ws2_raw), 0)
 
         gain = tile("gain", [P, PACK], F32, tag="w1_then_gain")

from contextlib import ExitStack

import concourse.mybir as mybir

K, T, S, H = 512, 2048, 512, 512
FLOPS = 4 * 2 * 512 * 512 * 512

F32 = mybir.dt.float32
BF16 = mybir.dt.bfloat16
I32 = mybir.dt.int32
U32 = mybir.dt.uint32
U16 = mybir.dt.uint16
U8 = mybir.dt.uint8
FP8X4 = mybir.dt.float8_e4m3fn_x4
ACT = mybir.ActivationFunctionType
ALU = mybir.AluOpType

P = 128
PACK = 4
MIX_CHUNKS = [(0, 256), (256, 256)]
OUT_CHUNKS = [(0, 128), (128, 128), (256, 128), (384, 128)]
STATES_ON_VECTOR = 0
PARTNERS_ON_SCALAR = 0
GROUP = (2, 2)
SPLIT = (1, 2)
LEAD = 1
OWN_ON_SCALAR = 2
OWN_ON_VECTOR = 4
MOVES_ON_VECTOR = (1, 1, 1, 1)
ROUNDINGS_ON_VECTOR = 1


def tile_picked_softswap_none_po_kernel(
    tc, x_words, x_scales, w1_words, w1_scales, w2_words, w2_scales, gn, w3_words, w3_scales,
    res, w4_words, w4_scales, offs, two, pt, mv, out_0, out_1, out_2,
):
    nc = tc.nc
    with ExitStack() as ctx:
        lists = ctx.enter_context(tc.tile_pool(name="lists", bufs=1))
        sb = ctx.enter_context(tc.tile_pool(name="sb", bufs=1))
        shared = ctx.enter_context(tc.tile_pool(name="shared", bufs=1))
        psum = ctx.enter_context(tc.psum_pool(name="psum", bufs=1))

        def tile(name, shape, dtype, tag=None):
            return sb.tile(shape, dtype, name=name, tag=tag or name, align_bytes=64)

        def placed(name, shape, dtype, offset):
            return shared.tile(shape, dtype, name=name, offset=offset, align_bytes=64)

        def load_list(name, source):
            held = lists.tile([P, S // 16], U16, name=name)
            nc.sync.dma_start(held[:], source)
            return held

        def load_words(queue, name, source, width, tag):
            held = tile(name, [P, width], U32, tag=tag)
            queue.dma_start(held[:].bitcast(I32), source[0].rearrange("p n t -> p (n t)").bitcast(I32))
            return held

        def load_scale_rows(queues, held, first_row, source):
            for quad, queue in enumerate(queues):
                row = 32 * quad + first_row
                queue.dma_start(held[row : row + 4, :].bitcast(I32), source[0, 4 * quad : 4 * quad + 4, :].bitcast(I32))

        def deal_words(name, raw):
            dealt = tile(name, [P, H], U32)
            nc.scalar.copy(
                dealt[:].rearrange("p (t b i) -> p b t i", t=PACK, i=4),
                raw[:].rearrange("p (b i t) -> p b t i", t=PACK, i=4),
            )
            return dealt

        def deal_scales(name, raw):
            dealt = tile(name, [P, H], U8)
            nc.vector.tensor_copy(
                dealt[:].rearrange("p (t m) -> p t m", t=PACK), raw[:].rearrange("p (m t) -> p t m", t=PACK)
            )
            return dealt

        def product(out, weight, t, codes, scales):
            words, plane, first_row = weight
            cols = slice(t * P, (t + 1) * P)
            nc.tensor.matmul_mx(
                out=out, lhsT=words[:, cols].bitcast(FP8X4), lhsT_scale=plane[first_row:P, cols],
                rhs=codes.bitcast(FP8X4), rhs_scale=scales, start=True, stop=True,
            )

        def woven(rounded):
            return rounded[:].rearrange("p (c i t) -> p c t i", i=2, t=PACK)

        def by_pairs(planes):
            return planes[:].rearrange("p t (c i) -> p c t i", i=2)

        def entries(held, first, width):
            return held[:, first // 16 : (first + width) // 16]

        xs_raw = tile("xs_raw", [P, T], U8)
        ws1_raw = tile("ws1_raw", [P, H], U8, tag="ws1_then_words_c")
        ws2_raw = tile("ws2_raw", [P, H], U8, tag="ws2_own_res")
        nc.gpsimd.memset(xs_raw[:, : T // 2].bitcast(I32), 0)
        nc.vector.memset(xs_raw[:, T // 2 :].bitcast(I32), 0)
        nc.gpsimd.memset(ws1_raw[:].bitcast(I32), 0)
        nc.gpsimd.memset(ws2_raw[:].bitcast(I32), 0)
        offs_t = load_list("offs_t", offs)
        two_t = load_list("two_t", two)
        pt_t = load_list("pt_t", pt)
        load_scale_rows([nc.sync] * 4, xs_raw, 0, x_scales)
        xw_raw = load_words(nc.sync, "xw_raw", x_words, T, "xw_raw")
        mv_t = load_list("mv_t", mv)
        w1_raw = load_words(nc.sync, "w1_raw", w1_words, H, "w1_then_gain")
        load_scale_rows([nc.sync] * 4, ws1_raw, 0, w1_scales)
        w2_raw = load_words(nc.sync, "w2_raw", w2_words, H, "w2_raw")
        load_scale_rows([nc.sync] * 4, ws2_raw, 0, w2_scales)

        xs_y = tile("xs_y", [P, S], U8, tag="xs_y_then_ws34")
        xw_y = tile("xw_y", [P, S], U32, tag="words_y")
        xs_c = tile("xs_c", [P, S], U8)
        nc.vector.tensor_copy(xs_y[:], xs_raw[:].indirect(offs_t[:]))
        nc.vector.tensor_copy(xs_c[:], xs_raw[:].indirect(two_t[:]))
        nc.vector.tensor_copy(xw_y[:], xw_raw[:].indirect(offs_t[:]))
        w1 = (deal_words("w1_d", w1_raw), deal_scales("ws1", ws1_raw), 0)
        xw_c = tile("xw_c", [P, S], U32, tag="ws1_then_words_c")
        nc.vector.tensor_copy(xw_c[:], xw_raw[:].indirect(two_t[:]))
        w2 = (deal_words("w2_d", w2_raw), deal_scales("ws2", ws2_raw), 0)

        gain = tile("gain", [P, PACK], F32, tag="w1_then_gain")
        nc.sync.dma_start(gain[:], gn.rearrange("(p t) o -> p (t o)", t=PACK))
        half_gain = tile("half_gain", [P, PACK], F32)
        nc.scalar.activation(half_gain[:], gain[:], ACT.Copy, scale=0.5)

        y_ps = [psum.tile([P, S], F32, name=f"y_ps{t}", tag=f"bank_y{t}") for t in range(PACK)]
        c_ps = [psum.tile([P, S], F32, name=f"c_ps{t}", tag=f"bank_c{t}") for t in range(PACK)]
        for t in range(PACK):
            product(y_ps[t][:], w1, t, xw_y[:], xs_y[:])
        for t in range(PACK):
            product(c_ps[t][:], w2, t, xw_c[:], xs_c[:])

        w3_raw = load_words(nc.sync, "w3_raw", w3_words, H, "words_y")
        ws34_raw = tile("ws34_raw", [P, H], U8, tag="xs_y_then_ws34")
        nc.vector.memset(ws34_raw[:].bitcast(I32), 0)
        load_scale_rows([nc.sync] * 4, ws34_raw, 0, w3_scales)
        load_scale_rows([nc.sync] * 4, ws34_raw, 4, w4_scales)
        y_win = [tile(f"y_win{t}", [P, S], F32) for t in range(PACK)]
        c_win = [tile(f"c_win{t}", [P, S], F32) for t in range(PACK)]
        h_win = [tile(f"h_win{t}", [P, S], F32) for t in range(PACK)]
        y_own = tile("y_own", [P, PACK, S], F32, tag="ws2_own_res")
        a_ps = {}
        w3 = None
        w4 = None

        partner_c, gap, pull = {}, {}, {}

        def look_up(n, t):
            first, width = MIX_CHUNKS[n]
            if t == 0:
                partner_c[n] = tile(f"partner_c{n}", [P, PACK, width], F32)
                gap[n] = tile(f"gap{n}", [P, PACK, width], F32)
                pull[n] = tile(f"pull{n}", [P, PACK, width], F32)
            partners = entries(pt_t, first, width)
            own = y_own[:, t, first : first + width]
            nc.vector.tensor_tensor(gap[n][:, t, :], y_win[t][:].indirect(partners), own, ALU.subtract)
            if (t + 1) % GROUP[n] == 0:
                group = slice(t + 1 - GROUP[n], t + 1)
                nc.scalar.activation(pull[n][:, group, :], gap[n][:, group, :], ACT.Tanh)
            nc.scalar.activation(partner_c[n][:, t, :], c_win[t][:].indirect(partners), ACT.Copy)

        taken, kept = {}, {}

        def weigh(n, t):
            first, width = MIX_CHUNKS[n]
            if t == 0:
                taken[n] = tile(f"taken{n}", [P, PACK, width], F32)
                kept[n] = tile(f"kept{n}", [P, PACK, width], F32)
            nc.vector.scalar_tensor_tensor(
                kept[n][:, t, :], pull[n][:, t, :], 1.0, c_win[t][:, first : first + width], ALU.add, ALU.mult
            )
            if (t + 1) % GROUP[n] == 0:
                group = slice(t + 1 - GROUP[n], t + 1)
                nc.vector.scalar_tensor_tensor(
                    taken[n][:, group, :], pull[n][:, group, :], 1.0, partner_c[n][:, group, :], ALU.subtract, ALU.mult
                )

        pieces = []

        def mix(n):
            first, width = MIX_CHUNKS[n]
            part = width // SPLIT[n]
            rounded = []
            for start in range(0, width, part):
                z_bf = tile(f"z_bf{first + start}", [P, PACK * part], BF16)
                within = slice(start // 2, (start + part) // 2)
                nc.vector.tensor_tensor(
                    woven(z_bf), by_pairs(kept[n])[:, within], by_pairs(taken[n])[:, within], ALU.subtract
                )
                rounded.append(z_bf)
            for z_bf, start in zip(rounded, range(first, first + width, part)):
                z_words = tile(f"z_words{start}", [P, part], U32)
                z_scales = tile(f"z_scales{start}", [P, part], U8)
                nc.vector.quantize_mx(out=z_words[:].bitcast(FP8X4), scales=z_scales[:], in_=z_bf[:])
                piece = len(pieces)
                pieces.append((start, part))
                for t in range(PACK):
                    bank = f"bank_c{t}" if piece % 2 == 0 else f"bank_y{t}"
                    a_ps[piece, t] = psum.tile([P, part], F32, name=f"a_ps{piece}_{t}", tag=bank)
                    product(a_ps[piece, t][:], w3, t, z_words[:], z_scales[:])

        for t in range(PACK):
            nc.scalar.copy(y_win[t][:], y_ps[t][:])
        for t in range(PACK):
            if t >= PACK - OWN_ON_SCALAR:
                nc.scalar.copy(y_own[:, t, :], y_ps[t][:])
            else:
                nc.vector.tensor_copy(y_own[:, t, :], y_win[t][:])
        units = [(n, t) for n in range(len(MIX_CHUNKS)) for t in range(PACK)]
        for step in range(len(units) + LEAD):
            if step < PACK:
                nc.scalar.activation(c_win[step][:], c_ps[step][:], ACT.Copy, scale=half_gain[:, step : step + 1])
            if step < len(units):
                look_up(*units[step])
            if step == PACK:
                ws34 = deal_scales("ws34", ws34_raw)
                w3 = (deal_words("w3_d", w3_raw), ws34, 0)
            if step >= LEAD:
                n, t = units[step - LEAD]
                weigh(n, t)
                if t == PACK - 1:
                    mix(n)
        for n, (first, width) in enumerate(pieces):
            cols = slice(first, first + width)
            for t in range(PACK):
                nc.scalar.activation(h_win[t][:, cols], a_ps[n, t][:], ACT.Tanh)
                if n == 0:
                    nc.scalar.activation(h_win[t][:, cols], h_win[t][:, cols], ACT.Copy, scale=gain[:, t : t + 1])
                if n == len(pieces) - 1:
                    late = slice(pieces[1][0], S)
                    nc.vector.tensor_scalar(h_win[t][:, late], h_win[t][:, late], gain[:, t : t + 1], None, ALU.mult)
            if n == 0:
                w4_raw = load_words(nc.sync, "w4_raw", w4_words, H, "words_y")
                w4 = (deal_words("w4_d", w4_raw), ws34, 4)

        res_t = tile("res_t", [P, PACK, S], F32, tag="ws2_own_res")
        nc.sync.dma_start(res_t[:], res.rearrange("(p t) j -> p t j", t=PACK))
        out_rows = out_0.rearrange("(p t) j -> p t j", t=PACK)
        out_words = out_1[0].rearrange("p n t -> p (n t)").bitcast(I32)
        o_ps = {}
        o_words = tile("o_words", [P, S], U32)
        o_scales = tile("o_scales", [P, S], U8)
        for n, (first, width) in enumerate(OUT_CHUNKS):
            cols = slice(first, first + width)
            moved = tile(f"moved{n}", [P, PACK, width], F32)
            for t in range(PACK):
                looked_up = h_win[t][:].indirect(entries(mv_t, first, width))
                if t < MOVES_ON_VECTOR[n]:
                    nc.vector.tensor_copy(moved[:, t, :], looked_up)
                else:
                    nc.scalar.activation(moved[:, t, :], looked_up, ACT.Copy)
            z2_bf = tile(f"z2_bf{n}", [P, PACK * width], BF16)
            nc.vector.tensor_copy(woven(z2_bf), by_pairs(moved))
            z2_words = tile(f"z2_words{n}", [P, width], U32)
            z2_scales = tile(f"z2_scales{n}", [P, width], U8)
            nc.vector.quantize_mx(out=z2_words[:].bitcast(FP8X4), scales=z2_scales[:], in_=z2_bf[:])
            halves = max(1, width // P)
            per = PACK // halves
            for half in range(halves):
                o_ps[n, half] = psum.tile([P, per, width], F32, name=f"o_ps{n}_{half}", tag=f"bank_y{(first // P + half) % PACK}")
                for t in range(per):
                    product(o_ps[n, half][:, t, :], w4, half * per + t, z2_words[:], z2_scales[:])
        for n, (first, width) in enumerate(OUT_CHUNKS):
            cols = slice(first, first + width)
            halves = max(1, width // P)
            per = PACK // halves
            result = tile(f"result{n}", [P, PACK, width], F32)
            for half in range(halves):
                rows = slice(half * per, (half + 1) * per)
                nc.vector.tensor_tensor(result[:, rows, :], o_ps[n, half][:], res_t[:, rows, cols], ALU.add)
            nc.sync.dma_start(out_rows[:, :, cols], result[:])
            o_bf = tile(f"o_bf{n}", [P, PACK * width], BF16)
            if n >= len(OUT_CHUNKS) - ROUNDINGS_ON_VECTOR:
                nc.vector.tensor_copy(woven(o_bf), by_pairs(result))
            else:
                nc.scalar.copy(woven(o_bf), by_pairs(result))
            nc.vector.quantize_mx(out=o_words[:, cols].bitcast(FP8X4), scales=o_scales[:, cols], in_=o_bf[:])
            if n >= len(OUT_CHUNKS) - 2:
                stored = slice(first if n == len(OUT_CHUNKS) - 1 else 0, first + width)
                nc.sync.dma_start(out_words[:, stored], o_words[:, stored].bitcast(I32))
        for quad in range(4):
            queue = nc.scalar if quad % 2 else nc.sync
            queue.dma_start(
                out_2[0, 4 * quad : 4 * quad + 4, :].bitcast(I32), o_scales[32 * quad : 32 * quad + 4, :].bitcast(I32)
            )
